import numpy as np
import ml_dtypes


def mxq(x, axis, fmt="e4m3"):
    dtype, down = {"e4m3": (ml_dtypes.float8_e4m3fn, 7), "e5m2": (ml_dtypes.float8_e5m2, 14)}[fmt]
    v = np.moveaxis(np.asarray(x, np.float32).astype(ml_dtypes.bfloat16).astype(np.float64), axis, -1)
    blocks = v.reshape(v.shape[:-1] + (-1, 32))
    amax = np.abs(blocks).max(-1, keepdims=True)
    byte = np.maximum(np.where(amax > 0, np.frexp(amax)[1] - 1 + 127, 0) - down, 1)
    scale = np.exp2(byte - 127.0)
    codes = (blocks / scale).astype(np.float32).astype(dtype).astype(np.float64)
    return np.moveaxis((codes * scale).reshape(v.shape), -1, axis)


WIDE = False


def mx_kscale(k):
    if not WIDE:
        return np.ones(k)
    levels = np.array([10, -10, 5, -5, 0])
    if k % 512:
        return np.exp2(np.random.permutation(np.resize(levels, k // 32))).repeat(32)
    a = np.empty((k // 512, 16))
    for p in range(k // 512):
        a[p, :8] = np.random.permutation(np.resize(levels, 8))
        for g in range(8):
            far = levels[np.abs(levels - a[p, g]) >= 10]
            a[p, g + 8] = far[np.random.randint(len(far))]
    return np.exp2(a.ravel()).repeat(32)


def f64(x):
    return np.asarray(x).astype(np.float64)


def striped(idx):
    return np.tile(idx.reshape(-1, 16).T, (8, 1)).astype(np.uint16)


def unstriped(offs):
    return offs[:16].T.reshape(-1).astype(np.int64)


E2M1 = np.array([0.0, 0.5, 1.0, 1.5, 2.0, 3.0, 4.0, 6.0, -0.0, -0.5, -1.0, -1.5, -2.0, -3.0, -4.0, -6.0])


def pack_weight(w, fmt):
    k, n = w.shape
    w = f64(np.asarray(w, np.float32).astype(ml_dtypes.bfloat16)).reshape(k // 32, 32, n)
    amax = np.abs(w).max(1)
    if fmt == "e4m3":
        byte = np.frexp(amax)[1] - 1 + 127 - 7
    else:
        mant, ex = np.frexp(amax / 6.0)
        byte = np.where(mant > 0.5, ex, ex - 1) + 127
    byte = np.clip(np.where(amax > 0, byte, 1), 1, 254)
    scaled = (w * np.exp2(127.0 - byte)[:, None, :]).reshape(k, n).astype(np.float32)
    by_word = np.ascontiguousarray(scaled.reshape(k // 512, 128, 4, n).transpose(0, 1, 3, 2))
    if fmt == "e4m3":
        words = by_word.astype(ml_dtypes.float8_e4m3fn).view(np.uint8)
    else:
        c = by_word.astype(ml_dtypes.float4_e2m1fn).view(np.uint8) & 0xF
        words = (c[..., 0::2] | (c[..., 1::2] << 4)).reshape(k // 512, 128, 2 * n)
    return np.ascontiguousarray(words), np.ascontiguousarray(byte.astype(np.uint8).reshape(k // 512, 16, n))


def unpack_weight(words, scales, fmt):
    g, _, n = scales.shape
    words = np.ascontiguousarray(words).reshape(g, 128, n, -1)
    if fmt == "e4m3":
        vals = words.view(ml_dtypes.float8_e4m3fn).astype(np.float64)
    else:
        nib = np.empty((g, 128, n, 4), np.uint8)
        nib[..., 0::2] = words & 0xF
        nib[..., 1::2] = words >> 4
        vals = E2M1[nib]
    vals = vals * np.repeat(np.exp2(scales.astype(np.float64) - 127.0), 8, axis=1)[..., None]
    return vals.transpose(0, 1, 3, 2).reshape(g * 512, n)


def d_silu(v):
    s = 1.0 / (1.0 + np.exp(-np.maximum(v, -700.0)))
    return s * (1.0 + v * (1.0 - s))


def silu(v):
    return v / (1.0 + np.exp(-np.maximum(v, -700.0)))


K, T, E, C, H, N = 512, 512, 4, 256, 512, 1024


def by_expert(wq, xq):
    return np.concatenate([wq[e].T @ xq[:, e * C:(e + 1) * C] for e in range(E)], axis=1)


def setup_inputs():
    n = np.random.standard_normal
    s = mx_kscale(K)
    v = mx_kscale(N)
    u = mx_kscale(H)
    first = np.random.permutation(np.repeat(np.arange(E), T // E))
    second = (first + 1 + np.random.permutation(np.repeat(np.arange(E - 1), -(-T // (E - 1)))[:T])) % E
    while np.bincount(second, minlength=E).max() != T // E:
        load = np.bincount(second, minlength=E); hi, lo = int(load.argmax()), int(load.argmin())
        t = np.flatnonzero((second == hi) & (first != lo))[0]; second[t] = lo
    slot_token = np.empty(E * C, np.int64); pos = np.empty((2, T), np.int64); fill = np.zeros(E, np.int64)
    place = np.stack([np.random.permutation(C) for _ in range(E)])
    for r, deal in enumerate((first, second)):
        for t in np.random.permutation(T):
            e = deal[t]; j = e * C + place[e, fill[e]]; fill[e] += 1; slot_token[j] = t; pos[r, t] = j
    g = np.random.uniform(0.2, 0.8, T)
    w_slot = np.empty(E * C); w_slot[pos[0]] = g; w_slot[pos[1]] = 1.0 - g
    x = pack_weight(n((K, T)) * s[:, None], "e4m3")
    dy = pack_weight(n((N, T)) * v[:, None], "e4m3")
    m1 = n((E, K, H))
    m3 = n((E, K, H))
    w1 = [pack_weight(m, "e2m1") for m in m1 / np.sqrt(K) / s[None, :, None]]
    w3 = [pack_weight(m, "e2m1") for m in m3 / np.sqrt(K) / s[None, :, None]]
    w2t = [pack_weight(m, "e2m1") for m in n((E, N, H)) / np.sqrt(N) / v[None, :, None] * u]
    w1t = [pack_weight(m, "e2m1") for m in m1.transpose(0, 2, 1) / np.sqrt(H) / u[None, :, None]]
    w3t = [pack_weight(m, "e2m1") for m in m3.transpose(0, 2, 1) / np.sqrt(H) / u[None, :, None]]
    return {
        "x_words": x[0],
        "x_scales": x[1],
        "dy_words": dy[0],
        "dy_scales": dy[1],
        "w1_words": np.stack([m[0] for m in w1]),
        "w1_scales": np.stack([m[1] for m in w1]),
        "w3_words": np.stack([m[0] for m in w3]),
        "w3_scales": np.stack([m[1] for m in w3]),
        "w2t_words": np.stack([m[0] for m in w2t]),
        "w2t_scales": np.stack([m[1] for m in w2t]),
        "w1t_words": np.stack([m[0] for m in w1t]),
        "w1t_scales": np.stack([m[1] for m in w1t]),
        "w3t_words": np.stack([m[0] for m in w3t]),
        "w3t_scales": np.stack([m[1] for m in w3t]),
        "gate": (np.tile(w_slot, (128, 1))).astype(np.float32),
        "offs": striped(slot_token),
        "pos1": striped(pos[0]),
        "pos2": striped(pos[1]),
    }


def reference(x_words, x_scales, dy_words, dy_scales, w1_words, w1_scales, w3_words, w3_scales, w2t_words, w2t_scales, w1t_words, w1t_scales, w3t_words, w3t_scales, gate, offs, pos1, pos2):
    w1 = np.stack([unpack_weight(w1_words[e], w1_scales[e], "e2m1") for e in range(E)])
    w3 = np.stack([unpack_weight(w3_words[e], w3_scales[e], "e2m1") for e in range(E)])
    w2t = np.stack([unpack_weight(w2t_words[e], w2t_scales[e], "e2m1") for e in range(E)])
    w1t = np.stack([unpack_weight(w1t_words[e], w1t_scales[e], "e2m1") for e in range(E)])
    w3t = np.stack([unpack_weight(w3t_words[e], w3t_scales[e], "e2m1") for e in range(E)])
    idx = unstriped(offs)
    xq = unpack_weight(x_words, x_scales, "e4m3")[:, idx]
    gq = unpack_weight(dy_words, dy_scales, "e4m3")[:, idx]
    dh = f64(gate[:1]) * by_expert(w2t, gq)
    a1, a3 = by_expert(w1, xq), by_expert(w3, xq)
    dx = by_expert(w1t, mxq(dh * a3 * d_silu(a1), 0, "e4m3")) + by_expert(w3t, mxq(dh * silu(a1), 0, "e4m3"))
    out = dx[:, unstriped(pos1)] + dx[:, unstriped(pos2)]
    return out

@@ -1,0 +1,231 @@
+from contextlib import ExitStack
+
+import concourse.mybir as mybir
+from concourse.masks import make_identity
+
+K, T, E, C, H, N = 512, 512, 4, 256, 512, 1024
+S = E * C
+FLOPS = 2 * S * (2 * K * H + N * H + 2 * H * K)
+BYTES = 5238784
+
+F32 = mybir.dt.float32
+BF16 = mybir.dt.bfloat16
+I32 = mybir.dt.int32
+U32 = mybir.dt.uint32
+U16 = mybir.dt.uint16
+U8 = mybir.dt.uint8
+FP8X4 = mybir.dt.float8_e4m3fn_x4
+FP4X4 = mybir.dt.float4_e2m1fn_x4
+ACT = mybir.ActivationFunctionType
+ALU = mybir.AluOpType
+
+P = 128
+TILES = S // P
+DY_PASSES = N // 512
+K_BLOCKS = K // P
+
+
+def tile_moe_rec_glu_silu_kernel(
+    tc, x_words, x_scales, dy_words, dy_scales, w1_words, w1_scales, w3_words, w3_scales,
+    w2t_words, w2t_scales, w1t_words, w1t_scales, w3t_words, w3t_scales, gate, offs, pos1, pos2, out,
+):
+    nc = tc.nc
+    with ExitStack() as ctx:
+        keep = ctx.enter_context(tc.tile_pool(name="keep", bufs=1))
+        ring = ctx.enter_context(tc.tile_pool(name="ring", bufs=3))
+        psum = ctx.enter_context(tc.psum_pool(name="psum", bufs=1))
+
+        def held(name, cols, dtype):
+            return keep.tile([P, cols], dtype, name=name, align_bytes=64)
+
+        def zeroed_plane(name, passes):
+            plane = held(name, passes * 512, U8)
+            nc.vector.memset(plane[:].bitcast(I32), 0)
+            return plane
+
+        def load_scales(plane, scales):
+            for r in range(4):
+                nc.sync.dma_start(
+                    out=plane[r:P:32, :].bitcast(I32).rearrange("q (g n) -> q g n", n=128),
+                    in_=scales[:, r:16:4, :].bitcast(I32).rearrange("g q n -> q g n"),
+                )
+
+        def load_words(name, words):
+            passes = words.shape[0]
+            tile = held(name, passes * 1024, U8)
+            nc.sync.dma_start(
+                out=tile[:].bitcast(I32).rearrange("p (g n) -> p g n", n=256),
+                in_=words.bitcast(I32).rearrange("g p n -> p g n"),
+            )
+            return tile
+
+        def by_pass(packed):
+            return packed.rearrange("e s a n -> (e s) a n")
+
+        xs = zeroed_plane("xs", 1)
+        dys = zeroed_plane("dys", DY_PASSES)
+        w1s = zeroed_plane("w1s", E)
+        w3s = zeroed_plane("w3s", E)
+        w2s = zeroed_plane("w2s", E * DY_PASSES)
+        w1ts = zeroed_plane("w1ts", E)
+        w3ts = zeroed_plane("w3ts", E)
+
+        ident = held("ident", P, F32)
+        make_identity(nc, ident[:])
+        gate_rows = held("gate_rows", P, F32)
+        nc.gpsimd.memset(gate_rows[:], 0.0)
+
+        offs_sb = keep.tile([P, S // 16], U16, name="offs_sb")
+        nc.sync.dma_start(offs_sb[:], offs)
+        xw = held("xw", T, I32)
+        nc.sync.dma_start(out=xw[:], in_=x_words[0].rearrange("p t d -> p (t d)").bitcast(I32))
+        load_scales(xs, x_scales)
+        dyw = []
+        for s in range(DY_PASSES):
+            dyw.append(held("dyw%d" % s, T, I32))
+            nc.sync.dma_start(out=dyw[s][:], in_=dy_words[s].rearrange("p t d -> p (t d)").bitcast(I32))
+        load_scales(dys, dy_scales)
+        load_scales(w1s, by_pass(w1_scales))
+        w1w = load_words("w1w", by_pass(w1_words))
+        load_scales(w3s, by_pass(w3_scales))
+        load_scales(w2s, by_pass(w2t_scales))
+        w3w = load_words("w3w", by_pass(w3_words))
+        w2w = [load_words("w2w%d" % a, by_pass(w2t_words)[4 * a : 4 * a + 4]) for a in range(2)]
+        nc.sync.dma_start(out=gate_rows[0:TILES, :], in_=gate[0].rearrange("(j p) -> j p", p=P))
+        load_scales(w1ts, by_pass(w1t_scales))
+        load_scales(w3ts, by_pass(w3t_scales))
+        w1tw = load_words("w1tw", by_pass(w1t_words))
+        w3tw = load_words("w3tw", by_pass(w3t_words))
+        pos1_sb = keep.tile([P, T // 16], U16, name="pos1_sb")
+        nc.sync.dma_start(pos1_sb[:], pos1)
+        pos2_sb = keep.tile([P, T // 16], U16, name="pos2_sb")
+        nc.sync.dma_start(pos2_sb[:], pos2)
+
+        def gathered(name, window, dtype, e):
+            tile = held(name, C, dtype)
+            nc.vector.tensor_copy(tile[:], window.indirect(offs_sb[:, e * C // 16 : (e + 1) * C // 16]))
+            return tile
+
+        xg, xsg, dyg, dysg = [], [], [], []
+        for e in range(E):
+            xg.append(gathered("xg%d" % e, xw[:].bitcast(U32), U32, e))
+            xsg.append(gathered("xsg%d" % e, xs[:], U8, e))
+        for e in range(E):
+            dyg.append([gathered("dyg%d_%d" % (e, s), dyw[s][:].bitcast(U32), U32, e) for s in range(DY_PASSES)])
+            dysg.append([gathered("dysg%d_%d" % (e, s), dys[:, s * T : (s + 1) * T], U8, e) for s in range(DY_PASSES)])
+
+        def first_product(bank, codes, scales, j, words, plane, g, start, stop):
+            cols = slice((j % 2) * P, (j % 2 + 1) * P)
+            nc.tensor.matmul_mx(
+                out=bank[:], lhsT=codes[:, cols].bitcast(FP8X4), lhsT_scale=scales[:, cols],
+                rhs=words.bitcast(FP4X4), rhs_scale=plane[:, g * 512 : (g + 1) * 512], start=start, stop=stop,
+            )
+
+        silu, sneg = [], []
+        for j in range(TILES):
+            e = j // 2
+            a1 = psum.tile([P, H], F32, name="a1", tag="a1", bufs=2)
+            first_product(a1, xg[e], xsg[e], j, w1w[:, e * 1024 : (e + 1) * 1024], w1s, e, True, True)
+            silu.append(held("silu%d" % j, H, F32))
+            nc.scalar.activation(silu[j][:], a1[:], ACT.Silu)
+            th = ring.tile([P, H], F32, name="th")
+            nc.scalar.activation(th[:], a1[:], ACT.Tanh, scale=0.5)
+            sneg.append(held("sneg%d" % j, H, F32))
+            nc.scalar.activation(sneg[j][:], th[:], ACT.Copy, scale=-0.5, bias=0.5)
+
+        gate_ps = psum.tile([P, 4, P], F32, name="gate_ps", tag="turn", bufs=2)
+        nc.tensor.transpose(gate_ps[:, 0, :], gate_rows[:], ident[:])
+        gate_col = held("gate_col", TILES, F32)
+        nc.scalar.copy(gate_col[:], gate_ps[:, 0, 0:TILES])
+
+        dx = [held("dx%d" % b, S, F32) for b in range(K_BLOCKS)]
+        slope, grouped = {}, {}
+
+        def make_slope(j):
+            slope[j] = ring.tile([P, H], F32, name="slope")
+            nc.vector.scalar_tensor_tensor(slope[j][:], silu[j][:], -1.0, sneg[j][:], ALU.add, ALU.mult)
+
+        def make_da(j):
+            e = j // 2
+            a3 = psum.tile([P, H], F32, name="a3", tag="a3")
+            first_product(a3, xg[e], xsg[e], j, w3w[:, e * 1024 : (e + 1) * 1024], w3s, e, True, True)
+            dh = psum.tile([P, H], F32, name="dh", tag="dh", bufs=2)
+            for s in range(DY_PASSES):
+                g = e * DY_PASSES + s
+                first_product(dh, dyg[e][s], dysg[e][s], j, w2w[g // 4][:, (g % 4) * 1024 : (g % 4 + 1) * 1024], w2s, g,
+                              s == 0, s == DY_PASSES - 1)
+            up = ring.tile([P, H], F32, name="up")
+            nc.vector.scalar_tensor_tensor(up[:], slope[j][:], 1.0, a3[:], ALU.add, ALU.mult)
+            da3 = ring.tile([P, H], BF16, name="da3")
+            nc.vector.scalar_tensor_tensor(da3[:], dh[:], gate_col[:, j : j + 1], silu[j][:], ALU.mult, ALU.mult)
+            da1 = ring.tile([P, H], BF16, name="da1")
+            nc.vector.scalar_tensor_tensor(da1[:], dh[:], gate_col[:, j : j + 1], up[:], ALU.mult, ALU.mult)
+            parts = [[da3], [da1]] if j == TILES - 1 else [[da3, da1]]
+            grouped[j] = [turn_and_group(part) for part in parts]
+
+        def turn_and_group(part):
+            n = len(part)
+            turn = psum.tile([P, 2 * n, P], F32, name="turn", tag="turn", bufs=2)
+            for w, da in enumerate(part):
+                for u in range(2):
+                    nc.tensor.transpose(turn[:, 2 * w + u, :], da[:].bitcast(F32)[:, u : H // 2 : 2], ident[:])
+            group = ring.tile([P, n * 4 * P], BF16, name="group", align_bytes=64)
+            nc.scalar.copy(
+                group[:].bitcast(F32).rearrange("p (w s u) -> p w s u", w=n, u=2),
+                turn[:].rearrange("p (w u) s -> p w s u", u=2),
+            )
+            return group
+
+        def second_product(j):
+            e = j // 2
+            operands = []
+            for group in grouped[j]:
+                width = group.shape[1] // 4
+                codes = ring.tile([P, width], U32, name="codes", align_bytes=64)
+                scales = ring.tile([P, width], U8, name="scales", align_bytes=64)
+                nc.vector.quantize_mx(out=codes[:].bitcast(FP8X4), scales=scales[:], in_=group[:])
+                operands.extend((codes[:, c : c + P], scales[:, c : c + P]) for c in range(0, width, P))
+            if j == TILES - 1:
+                sums = [psum.tile([P, P], F32, name="last", tag=tag, bufs=bufs)[:]
+                        for tag, bufs in (("a1", 2), ("a1", 2), ("a3", 1), ("dxp", 1))]
+            else:
+                bank = psum.tile([P, K], F32, name="dxp", tag="dxp")
+                sums = [bank[:, b * P : (b + 1) * P] for b in range(K_BLOCKS)]
+            for b in range(K_BLOCKS):
+                for w, (words, plane) in enumerate(((w3tw, w3ts), (w1tw, w1ts))):
+                    nc.tensor.matmul_mx(
+                        out=sums[b],
+                        lhsT=words[:, e * 1024 + b * 256 : e * 1024 + (b + 1) * 256].bitcast(FP4X4),
+                        lhsT_scale=plane[:, e * 512 + b * P : e * 512 + (b + 1) * P],
+                        rhs=operands[w][0].bitcast(FP8X4), rhs_scale=operands[w][1],
+                        start=(w == 0), stop=(w == 1),
+                    )
+            for b in range(K_BLOCKS):
+                nc.scalar.copy(dx[b][:, j * P : (j + 1) * P], sums[b])
+
+        make_slope(0)
+        for j in range(TILES):
+            make_da(j)
+            if j + 1 < TILES:
+                make_slope(j + 1)
+            if j > 0:
+                second_product(j - 1)
+        second_product(TILES - 1)
+
+        first = []
+
+        def fetch_first(b):
+            first.append(held("first%d" % b, T, F32))
+            nc.vector.tensor_copy(first[b][:], dx[b][:].indirect(pos1_sb[:]))
+
+        fetch_first(0)
+        for b in range(K_BLOCKS):
+            if b + 1 < K_BLOCKS:
+                fetch_first(b + 1)
+            pieces = 2 if b == K_BLOCKS - 1 else 1
+            width = T // pieces
+            for c in range(0, T, width):
+                total = held("total%d_%d" % (b, c), width, F32)
+                nc.vector.tensor_tensor(total[:], dx[b][:].indirect(pos2_sb[:, c // 16 : (c + width) // 16]),
+                                        first[b][:, c : c + width], ALU.add)
+                nc.sync.dma_start(out=out[b * P : (b + 1) * P, c : c + width], in_=total[:])

@@ -23,6 +23,7 @@ P = 128
 TILES = S // P
 DY_PASSES = N // 512
 K_BLOCKS = K // P
+AHEAD = 3
 
 
 def tile_moe_rec_glu_silu_kernel(
@@ -38,9 +39,9 @@ def tile_moe_rec_glu_silu_kernel(
         def held(name, cols, dtype):
             return keep.tile([P, cols], dtype, name=name, align_bytes=64)
 
-        def zeroed_plane(name, passes):
+        def zeroed_plane(name, passes, engine):
             plane = held(name, passes * 512, U8)
-            nc.vector.memset(plane[:].bitcast(I32), 0)
+            engine.memset(plane[:].bitcast(I32), 0)
             return plane
 
         def load_scales(plane, scales):
@@ -62,18 +63,17 @@ def tile_moe_rec_glu_silu_kernel(
         def by_pass(packed):
             return packed.rearrange("e s a n -> (e s) a n")
 
-        xs = zeroed_plane("xs", 1)
-        dys = zeroed_plane("dys", DY_PASSES)
-        w1s = zeroed_plane("w1s", E)
-        w3s = zeroed_plane("w3s", E)
-        w2s = zeroed_plane("w2s", E * DY_PASSES)
-        w1ts = zeroed_plane("w1ts", E)
-        w3ts = zeroed_plane("w3ts", E)
-
-        ident = held("ident", P, F32)
-        make_identity(nc, ident[:])
+        xs = zeroed_plane("xs", 1, nc.vector)
+        dys = zeroed_plane("dys", DY_PASSES, nc.vector)
+        w1s = zeroed_plane("w1s", E, nc.vector)
+        w3s = zeroed_plane("w3s", E, nc.vector)
+        w2s = zeroed_plane("w2s", E * DY_PASSES, nc.gpsimd)
         gate_rows = held("gate_rows", P, F32)
         nc.gpsimd.memset(gate_rows[:], 0.0)
+        ident = held("ident", P, F32)
+        make_identity(nc, ident[:])
+        w1ts = zeroed_plane("w1ts", E, nc.gpsimd)
+        w3ts = zeroed_plane("w3ts", E, nc.gpsimd)
 
         offs_sb = keep.tile([P, S // 16], U16, name="offs_sb")
         nc.sync.dma_start(offs_sb[:], offs)
@@ -87,11 +87,30 @@ def tile_moe_rec_glu_silu_kernel(
         load_scales(dys, dy_scales)
         load_scales(w1s, by_pass(w1_scales))
         w1w = load_words("w1w", by_pass(w1_words))
-        load_scales(w3s, by_pass(w3_scales))
         load_scales(w2s, by_pass(w2t_scales))
-        w3w = load_words("w3w", by_pass(w3_words))
-        w2w = [load_words("w2w%d" % a, by_pass(w2t_words)[4 * a : 4 * a + 4]) for a in range(2)]
+        w2w = [load_words("w2w0", by_pass(w2t_words)[0:4])]
         nc.sync.dma_start(out=gate_rows[0:TILES, :], in_=gate[0].rearrange("(j p) -> j p", p=P))
+        w3w = load_words("w3w", by_pass(w3_words))
+        load_scales(w3s, by_pass(w3_scales))
+
+        def gathered(name, window, dtype, e, bufs):
+            tile = keep.tile([P, C], dtype, name=name, bufs=bufs, align_bytes=64)
+            nc.vector.tensor_copy(tile[:], window.indirect(offs_sb[:, e * C // 16 : (e + 1) * C // 16]))
+            return tile
+
+        xg, xsg, dyg, dysg = [], [], [], []
+        for e in range(E):
+            xg.append(gathered("xg", xw[:].bitcast(U32), U32, e, E))
+            xsg.append(gathered("xsg", xs[:], U8, e, E))
+
+        def gather_gradients(e):
+            dyg.append([gathered("dyg%d" % s, dyw[s][:].bitcast(U32), U32, e, 2) for s in range(DY_PASSES)])
+            dysg.append([gathered("dysg%d" % s, dys[:, s * T : (s + 1) * T], U8, e, 2) for s in range(DY_PASSES)])
+
+        gather_gradients(0)
+        gather_gradients(1)
+
+        w2w.append(load_words("w2w1", by_pass(w2t_words)[4:8]))
         load_scales(w1ts, by_pass(w1t_scales))
         load_scales(w3ts, by_pass(w3t_scales))
         w1tw = load_words("w1tw", by_pass(w1t_words))
@@ -101,19 +120,6 @@ def tile_moe_rec_glu_silu_kernel(
         pos2_sb = keep.tile([P, T // 16], U16, name="pos2_sb")
         nc.sync.dma_start(pos2_sb[:], pos2)
 
-        def gathered(name, window, dtype, e):
-            tile = held(name, C, dtype)
-            nc.vector.tensor_copy(tile[:], window.indirect(offs_sb[:, e * C // 16 : (e + 1) * C // 16]))
-            return tile
-
-        xg, xsg, dyg, dysg = [], [], [], []
-        for e in range(E):
-            xg.append(gathered("xg%d" % e, xw[:].bitcast(U32), U32, e))
-            xsg.append(gathered("xsg%d" % e, xs[:], U8, e))
-        for e in range(E):
-            dyg.append([gathered("dyg%d_%d" % (e, s), dyw[s][:].bitcast(U32), U32, e) for s in range(DY_PASSES)])
-            dysg.append([gathered("dysg%d_%d" % (e, s), dys[:, s * T : (s + 1) * T], U8, e) for s in range(DY_PASSES)])
-
         def first_product(bank, codes, scales, j, words, plane, g, start, stop):
             cols = slice((j % 2) * P, (j % 2 + 1) * P)
             nc.tensor.matmul_mx(
@@ -121,51 +127,57 @@ def tile_moe_rec_glu_silu_kernel(
                 rhs=words.bitcast(FP4X4), rhs_scale=plane[:, g * 512 : (g + 1) * 512], start=start, stop=stop,
             )
 
-        silu, sneg = [], []
-        for j in range(TILES):
-            e = j // 2
-            a1 = psum.tile([P, H], F32, name="a1", tag="a1", bufs=2)
-            first_product(a1, xg[e], xsg[e], j, w1w[:, e * 1024 : (e + 1) * 1024], w1s, e, True, True)
-            silu.append(held("silu%d" % j, H, F32))
-            nc.scalar.activation(silu[j][:], a1[:], ACT.Silu)
-            th = ring.tile([P, H], F32, name="th")
-            nc.scalar.activation(th[:], a1[:], ACT.Tanh, scale=0.5)
-            sneg.append(held("sneg%d" % j, H, F32))
-            nc.scalar.activation(sneg[j][:], th[:], ACT.Copy, scale=-0.5, bias=0.5)
+        a1, silu_neg, sig_neg = {}, {}, {}
 
-        gate_ps = psum.tile([P, 4, P], F32, name="gate_ps", tag="turn", bufs=2)
+        def activations(j):
+            e = j // 2
+            a1[j] = psum.tile([P, H], F32, name="a1", tag="a1", bufs=AHEAD)
+            first_product(a1[j], xg[e], xsg[e], j, w1w[:, e * 1024 : (e + 1) * 1024], w1s, e, True, True)
+            silu_neg[j] = held("silu_neg%d" % j, H, F32)
+            nc.scalar.activation(silu_neg[j][:], a1[j][:], ACT.Silu, scale=-1.0)
+            th = ring.tile([P, H], F32, name="th")
+            nc.scalar.activation(th[:], a1[j][:], ACT.Tanh, scale=0.5)
+            sig_neg[j] = held("sig_neg%d" % j, H, F32)
+            nc.scalar.activation(sig_neg[j][:], th[:], ACT.Copy, scale=-0.5, bias=-0.5)
+
+        gate_ps = psum.tile([P, 4, P], F32, name="gate_ps", tag="turn")
         nc.tensor.transpose(gate_ps[:, 0, :], gate_rows[:], ident[:])
         gate_col = held("gate_col", TILES, F32)
-        nc.scalar.copy(gate_col[:], gate_ps[:, 0, 0:TILES])
+        nc.vector.tensor_copy(gate_col[:], gate_ps[:, 0, 0:TILES])
+
+        for j in range(AHEAD):
+            activations(j)
 
         dx = [held("dx%d" % b, S, F32) for b in range(K_BLOCKS)]
-        slope, grouped = {}, {}
+        dh_sig, grouped = {}, {}
 
-        def make_slope(j):
-            slope[j] = ring.tile([P, H], F32, name="slope")
-            nc.vector.scalar_tensor_tensor(slope[j][:], silu[j][:], -1.0, sneg[j][:], ALU.add, ALU.mult)
+        def make_dh_sig(j):
+            e = j // 2
+            dh = psum.tile([P, H], F32, name="dh", tag="dh")
+            for s in range(DY_PASSES):
+                g = e * DY_PASSES + s
+                first_product(dh, dyg[e][s], dysg[e][s], j, w2w[g // 4][:, (g % 4) * 1024 : (g % 4 + 1) * 1024], w2s, g,
+                              s == 0, s == DY_PASSES - 1)
+            dh_sig[j] = ring.tile([P, H], F32, name="dh_sig")
+            nc.vector.scalar_tensor_tensor(dh_sig[j][:], dh[:], gate_col[:, j : j + 1], sig_neg[j][:], ALU.mult, ALU.mult)
 
         def make_da(j):
             e = j // 2
             a3 = psum.tile([P, H], F32, name="a3", tag="a3")
             first_product(a3, xg[e], xsg[e], j, w3w[:, e * 1024 : (e + 1) * 1024], w3s, e, True, True)
-            dh = psum.tile([P, H], F32, name="dh", tag="dh", bufs=2)
-            for s in range(DY_PASSES):
-                g = e * DY_PASSES + s
-                first_product(dh, dyg[e][s], dysg[e][s], j, w2w[g // 4][:, (g % 4) * 1024 : (g % 4 + 1) * 1024], w2s, g,
-                              s == 0, s == DY_PASSES - 1)
             up = ring.tile([P, H], F32, name="up")
-            nc.vector.scalar_tensor_tensor(up[:], slope[j][:], 1.0, a3[:], ALU.add, ALU.mult)
+            nc.vector.scalar_tensor_tensor(up[:], silu_neg[j][:], -1.0, a3[:], ALU.add, ALU.mult)
             da3 = ring.tile([P, H], BF16, name="da3")
-            nc.vector.scalar_tensor_tensor(da3[:], dh[:], gate_col[:, j : j + 1], silu[j][:], ALU.mult, ALU.mult)
+            nc.vector.scalar_tensor_tensor(da3[:], a1[j][:], -1.0, dh_sig[j][:], ALU.mult, ALU.mult)
             da1 = ring.tile([P, H], BF16, name="da1")
-            nc.vector.scalar_tensor_tensor(da1[:], dh[:], gate_col[:, j : j + 1], up[:], ALU.mult, ALU.mult)
-            parts = [[da3], [da1]] if j == TILES - 1 else [[da3, da1]]
-            grouped[j] = [turn_and_group(part) for part in parts]
+            engine = nc.vector if j == TILES - 1 else nc.gpsimd
+            engine.tensor_tensor(da1[:], dh_sig[j][:], up[:], ALU.mult)
+            parts = [([da3], "dh"), ([da1], "turn")] if j == TILES - 1 else [([da3, da1], "turn")]
+            grouped[j] = [turn_and_group(part, tag) for part, tag in parts]
 
-        def turn_and_group(part):
+        def turn_and_group(part, tag):
             n = len(part)
-            turn = psum.tile([P, 2 * n, P], F32, name="turn", tag="turn", bufs=2)
+            turn = psum.tile([P, 2 * n, P], F32, name="turn", tag=tag)
             for w, da in enumerate(part):
                 for u in range(2):
                     nc.tensor.transpose(turn[:, 2 * w + u, :], da[:].bitcast(F32)[:, u : H // 2 : 2], ident[:])
@@ -187,9 +199,9 @@ def tile_moe_rec_glu_silu_kernel(
                 operands.extend((codes[:, c : c + P], scales[:, c : c + P]) for c in range(0, width, P))
             if j == TILES - 1:
                 sums = [psum.tile([P, P], F32, name="last", tag=tag, bufs=bufs)[:]
-                        for tag, bufs in (("a1", 2), ("a1", 2), ("a3", 1), ("dxp", 1))]
+                        for tag, bufs in (("a1", AHEAD), ("a1", AHEAD), ("a1", AHEAD), ("a3", 1))]
             else:
-                bank = psum.tile([P, K], F32, name="dxp", tag="dxp")
+                bank = psum.tile([P, K], F32, name="dxp", tag="dxp", bufs=2)
                 sums = [bank[:, b * P : (b + 1) * P] for b in range(K_BLOCKS)]
             for b in range(K_BLOCKS):
                 for w, (words, plane) in enumerate(((w3tw, w3ts), (w1tw, w1ts))):
@@ -203,13 +215,17 @@ def tile_moe_rec_glu_silu_kernel(
             for b in range(K_BLOCKS):
                 nc.scalar.copy(dx[b][:, j * P : (j + 1) * P], sums[b])
 
-        make_slope(0)
+        make_dh_sig(0)
         for j in range(TILES):
             make_da(j)
             if j + 1 < TILES:
-                make_slope(j + 1)
+                make_dh_sig(j + 1)
             if j > 0:
                 second_product(j - 1)
+            if j + AHEAD < TILES:
+                activations(j + AHEAD)
+            if j in (1, 3):
+                gather_gradients(j // 2 + 2)
         second_product(TILES - 1)
 
         first = []

@@ -23,7 +23,9 @@ P = 128
 TILES = S // P
 DY_PASSES = N // 512
 K_BLOCKS = K // P
-AHEAD = 3
+AHEAD = 6
+HALF = S // 2
+SPARE = 192
 
 
 def tile_moe_rec_glu_silu_kernel(
@@ -44,12 +46,13 @@ def tile_moe_rec_glu_silu_kernel(
             engine.memset(plane[:].bitcast(I32), 0)
             return plane
 
-        def load_scales(plane, scales):
+        def load_scales(*pairs):
             for r in range(4):
-                nc.sync.dma_start(
-                    out=plane[r:P:32, :].bitcast(I32).rearrange("q (g n) -> q g n", n=128),
-                    in_=scales[:, r:16:4, :].bitcast(I32).rearrange("g q n -> q g n"),
-                )
+                for plane, scales in pairs:
+                    nc.sync.dma_start(
+                        out=plane[r:P:32, :].bitcast(I32).rearrange("q (g n) -> q g n", n=128),
+                        in_=scales[:, r:16:4, :].bitcast(I32).rearrange("g q n -> q g n"),
+                    )
 
         def load_words(name, words):
             passes = words.shape[0]
@@ -63,56 +66,60 @@ def tile_moe_rec_glu_silu_kernel(
         def by_pass(packed):
             return packed.rearrange("e s a n -> (e s) a n")
 
-        xs = zeroed_plane("xs", 1, nc.vector)
-        dys = zeroed_plane("dys", DY_PASSES, nc.vector)
+        xs = zeroed_plane("xs", 2, nc.vector)
+        dys = zeroed_plane("dys", 4, nc.vector)
         w1s = zeroed_plane("w1s", E, nc.vector)
-        w3s = zeroed_plane("w3s", E, nc.vector)
-        w2s = zeroed_plane("w2s", E * DY_PASSES, nc.gpsimd)
+        xw = held("xw", T + SPARE, I32)
+        nc.vector.memset(xw[:, T:], 0)
+        dyw = [held("dyw%d" % s, T + SPARE, I32) for s in range(DY_PASSES)]
+        for tile in dyw:
+            nc.vector.memset(tile[:, T:], 0)
+        w3s = zeroed_plane("w3s", E, nc.gpsimd)
         gate_rows = held("gate_rows", P, F32)
         nc.gpsimd.memset(gate_rows[:], 0.0)
+        w2s = zeroed_plane("w2s", E * DY_PASSES, nc.gpsimd)
         ident = held("ident", P, F32)
         make_identity(nc, ident[:])
+        dysg1 = zeroed_plane("dysg1", 2, nc.gpsimd)
         w1ts = zeroed_plane("w1ts", E, nc.gpsimd)
         w3ts = zeroed_plane("w3ts", E, nc.gpsimd)
 
         offs_sb = keep.tile([P, S // 16], U16, name="offs_sb")
         nc.sync.dma_start(offs_sb[:], offs)
-        xw = held("xw", T, I32)
-        nc.sync.dma_start(out=xw[:], in_=x_words[0].rearrange("p t d -> p (t d)").bitcast(I32))
-        load_scales(xs, x_scales)
-        dyw = []
-        for s in range(DY_PASSES):
-            dyw.append(held("dyw%d" % s, T, I32))
-            nc.sync.dma_start(out=dyw[s][:], in_=dy_words[s].rearrange("p t d -> p (t d)").bitcast(I32))
-        load_scales(dys, dy_scales)
-        load_scales(w1s, by_pass(w1_scales))
+        nc.sync.dma_start(out=xw[:, 0:T], in_=x_words[0].rearrange("p t d -> p (t d)").bitcast(I32))
+        load_scales((xs[:, 0:T], x_scales))
+        for q in range(4):
+            nc.sync.dma_start(out=dys[32 * q : 32 * q + 8, 0:T].bitcast(I32),
+                              in_=dy_scales[:, 4 * q : 4 * q + 4, :].bitcast(I32))
+        load_scales((w1s, by_pass(w1_scales)))
         w1w = load_words("w1w", by_pass(w1_words))
-        load_scales(w2s, by_pass(w2t_scales))
-        w2w = [load_words("w2w0", by_pass(w2t_words)[0:4])]
-        nc.sync.dma_start(out=gate_rows[0:TILES, :], in_=gate[0].rearrange("(j p) -> j p", p=P))
         w3w = load_words("w3w", by_pass(w3_words))
-        load_scales(w3s, by_pass(w3_scales))
+        w2w = [load_words("w2w0", by_pass(w2t_words)[0:4])]
+        for s in range(DY_PASSES):
+            nc.sync.dma_start(out=dyw[s][:, 0:T], in_=dy_words[s].rearrange("p t d -> p (t d)").bitcast(I32))
+        nc.sync.dma_start(out=gate_rows[0:TILES, :], in_=gate[0].rearrange("(j p) -> j p", p=P))
+        load_scales((w3s, by_pass(w3_scales)))
+        load_scales((w2s, by_pass(w2t_scales)))
 
-        def gathered(name, window, dtype, e, bufs):
-            tile = keep.tile([P, C], dtype, name=name, bufs=bufs, align_bytes=64)
-            nc.vector.tensor_copy(tile[:], window.indirect(offs_sb[:, e * C // 16 : (e + 1) * C // 16]))
+        def gathered(name, window, dtype, first_slot, slots):
+            tile = held(name, slots, dtype)
+            nc.vector.tensor_copy(tile[:], window.indirect(offs_sb[:, first_slot // 16 : (first_slot + slots) // 16]))
             return tile
 
-        xg, xsg, dyg, dysg = [], [], [], []
-        for e in range(E):
-            xg.append(gathered("xg", xw[:].bitcast(U32), U32, e, E))
-            xsg.append(gathered("xsg", xs[:], U8, e, E))
-
-        def gather_gradients(e):
-            dyg.append([gathered("dyg%d" % s, dyw[s][:].bitcast(U32), U32, e, 2) for s in range(DY_PASSES)])
-            dysg.append([gathered("dysg%d" % s, dys[:, s * T : (s + 1) * T], U8, e, 2) for s in range(DY_PASSES)])
-
-        gather_gradients(0)
-        gather_gradients(1)
+        xg, xsg, dyg = [], [], []
+        for a in range(2):
+            xg.append(gathered("xg%d" % a, xw[:].bitcast(U32), U32, a * HALF, HALF))
+            xsg.append(gathered("xsg%d" % a, xs[:], U8, a * HALF, HALF))
+        dysg0 = gathered("dysg0", dys[:], U8, 0, S)
+        for r in range(4):
+            nc.sync.dma_start(out=dysg1[r:P:32, :].bitcast(I32), in_=dysg0[4 + r : P : 32, :].bitcast(I32))
+        for a in range(2):
+            dyg.append([gathered("dyg%d_%d" % (a, s), dyw[s][:].bitcast(U32), U32, a * HALF, HALF)
+                        for s in range(DY_PASSES)])
+        dysg = [[plane[:, a * HALF : (a + 1) * HALF] for plane in (dysg0, dysg1)] for a in range(2)]
 
         w2w.append(load_words("w2w1", by_pass(w2t_words)[4:8]))
-        load_scales(w1ts, by_pass(w1t_scales))
-        load_scales(w3ts, by_pass(w3t_scales))
+        load_scales((w1ts, by_pass(w1t_scales)), (w3ts, by_pass(w3t_scales)))
         w1tw = load_words("w1tw", by_pass(w1t_words))
         w3tw = load_words("w3tw", by_pass(w3t_words))
         pos1_sb = keep.tile([P, T // 16], U16, name="pos1_sb")
@@ -121,26 +128,26 @@ def tile_moe_rec_glu_silu_kernel(
         nc.sync.dma_start(pos2_sb[:], pos2)
 
         def first_product(bank, codes, scales, j, words, plane, g, start, stop):
-            cols = slice((j % 2) * P, (j % 2 + 1) * P)
+            cols = slice((j % 4) * P, (j % 4 + 1) * P)
             nc.tensor.matmul_mx(
                 out=bank[:], lhsT=codes[:, cols].bitcast(FP8X4), lhsT_scale=scales[:, cols],
                 rhs=words.bitcast(FP4X4), rhs_scale=plane[:, g * 512 : (g + 1) * 512], start=start, stop=stop,
             )
 
-        a1, silu_neg, sig_neg = {}, {}, {}
+        silu, sneg = {}, {}
 
         def activations(j):
             e = j // 2
-            a1[j] = psum.tile([P, H], F32, name="a1", tag="a1", bufs=AHEAD)
-            first_product(a1[j], xg[e], xsg[e], j, w1w[:, e * 1024 : (e + 1) * 1024], w1s, e, True, True)
-            silu_neg[j] = held("silu_neg%d" % j, H, F32)
-            nc.scalar.activation(silu_neg[j][:], a1[j][:], ACT.Silu, scale=-1.0)
+            a1 = psum.tile([P, H], F32, name="a1", tag="sums", bufs=2)
+            first_product(a1, xg[j // 4], xsg[j // 4], j, w1w[:, e * 1024 : (e + 1) * 1024], w1s, e, True, True)
+            silu[j] = held("silu%d" % j, H, F32)
+            nc.scalar.activation(silu[j][:], a1[:], ACT.Silu)
             th = ring.tile([P, H], F32, name="th")
-            nc.scalar.activation(th[:], a1[j][:], ACT.Tanh, scale=0.5)
-            sig_neg[j] = held("sig_neg%d" % j, H, F32)
-            nc.scalar.activation(sig_neg[j][:], th[:], ACT.Copy, scale=-0.5, bias=-0.5)
+            nc.scalar.activation(th[:], a1[:], ACT.Tanh, scale=0.5)
+            sneg[j] = held("sneg%d" % j, H, F32)
+            nc.scalar.activation(sneg[j][:], th[:], ACT.Copy, scale=-0.5, bias=0.5)
 
-        gate_ps = psum.tile([P, 4, P], F32, name="gate_ps", tag="turn")
+        gate_ps = psum.tile([P, 4, P], F32, name="gate_ps", tag="turn", bufs=2)
         nc.tensor.transpose(gate_ps[:, 0, :], gate_rows[:], ident[:])
         gate_col = held("gate_col", TILES, F32)
         nc.vector.tensor_copy(gate_col[:], gate_ps[:, 0, 0:TILES])
@@ -149,35 +156,33 @@ def tile_moe_rec_glu_silu_kernel(
             activations(j)
 
         dx = [held("dx%d" % b, S, F32) for b in range(K_BLOCKS)]
-        dh_sig, grouped = {}, {}
+        slope, grouped, last = {}, {}, []
 
-        def make_dh_sig(j):
-            e = j // 2
-            dh = psum.tile([P, H], F32, name="dh", tag="dh")
-            for s in range(DY_PASSES):
-                g = e * DY_PASSES + s
-                first_product(dh, dyg[e][s], dysg[e][s], j, w2w[g // 4][:, (g % 4) * 1024 : (g % 4 + 1) * 1024], w2s, g,
-                              s == 0, s == DY_PASSES - 1)
-            dh_sig[j] = ring.tile([P, H], F32, name="dh_sig")
-            nc.vector.scalar_tensor_tensor(dh_sig[j][:], dh[:], gate_col[:, j : j + 1], sig_neg[j][:], ALU.mult, ALU.mult)
+        def make_slope(j):
+            slope[j] = ring.tile([P, H], F32, name="slope")
+            nc.vector.scalar_tensor_tensor(slope[j][:], silu[j][:], -1.0, sneg[j][:], ALU.add, ALU.mult)
 
         def make_da(j):
             e = j // 2
-            a3 = psum.tile([P, H], F32, name="a3", tag="a3")
-            first_product(a3, xg[e], xsg[e], j, w3w[:, e * 1024 : (e + 1) * 1024], w3s, e, True, True)
+            a3 = psum.tile([P, H], F32, name="a3", tag="a3", bufs=2)
+            first_product(a3, xg[j // 4], xsg[j // 4], j, w3w[:, e * 1024 : (e + 1) * 1024], w3s, e, True, True)
+            dh = psum.tile([P, H], F32, name="dh", tag="dh", bufs=2)
+            for s in range(DY_PASSES):
+                g = e * DY_PASSES + s
+                first_product(dh, dyg[j // 4][s], dysg[j // 4][s], j, w2w[g // 4][:, (g % 4) * 1024 : (g % 4 + 1) * 1024],
+                              w2s, g, s == 0, s == DY_PASSES - 1)
             up = ring.tile([P, H], F32, name="up")
-            nc.vector.scalar_tensor_tensor(up[:], silu_neg[j][:], -1.0, a3[:], ALU.add, ALU.mult)
+            nc.vector.scalar_tensor_tensor(up[:], slope[j][:], 1.0, a3[:], ALU.add, ALU.mult)
             da3 = ring.tile([P, H], BF16, name="da3")
-            nc.vector.scalar_tensor_tensor(da3[:], a1[j][:], -1.0, dh_sig[j][:], ALU.mult, ALU.mult)
+            nc.vector.scalar_tensor_tensor(da3[:], dh[:], gate_col[:, j : j + 1], silu[j][:], ALU.mult, ALU.mult)
             da1 = ring.tile([P, H], BF16, name="da1")
-            engine = nc.vector if j == TILES - 1 else nc.gpsimd
-            engine.tensor_tensor(da1[:], dh_sig[j][:], up[:], ALU.mult)
-            parts = [([da3], "dh"), ([da1], "turn")] if j == TILES - 1 else [([da3, da1], "turn")]
-            grouped[j] = [turn_and_group(part, tag) for part, tag in parts]
+            nc.vector.scalar_tensor_tensor(da1[:], dh[:], gate_col[:, j : j + 1], up[:], ALU.mult, ALU.mult)
+            parts = [[da3], [da1]] if j == TILES - 1 else [[da3, da1]]
+            grouped[j] = [turn_and_group(part) for part in parts]
 
-        def turn_and_group(part, tag):
+        def turn_and_group(part):
             n = len(part)
-            turn = psum.tile([P, 2 * n, P], F32, name="turn", tag=tag)
+            turn = psum.tile([P, 2 * n, P], F32, name="turn", tag="turn", bufs=2)
             for w, da in enumerate(part):
                 for u in range(2):
                     nc.tensor.transpose(turn[:, 2 * w + u, :], da[:].bitcast(F32)[:, u : H // 2 : 2], ident[:])
@@ -197,11 +202,13 @@ def tile_moe_rec_glu_silu_kernel(
                 scales = ring.tile([P, width], U8, name="scales", align_bytes=64)
                 nc.vector.quantize_mx(out=codes[:].bitcast(FP8X4), scales=scales[:], in_=group[:])
                 operands.extend((codes[:, c : c + P], scales[:, c : c + P]) for c in range(0, width, P))
-            if j == TILES - 1:
-                sums = [psum.tile([P, P], F32, name="last", tag=tag, bufs=bufs)[:]
-                        for tag, bufs in (("a1", AHEAD), ("a1", AHEAD), ("a1", AHEAD), ("a3", 1))]
+            if e == E - 1:
+                if j % 2 == 0:
+                    last.extend(psum.tile([P, C], F32, name="last", tag=tag, bufs=bufs)
+                                for tag, bufs in (("a3", 2), ("a3", 2), ("dh", 2), ("sums", 2)))
+                sums = [bank[:, (j % 2) * P : (j % 2 + 1) * P] for bank in last]
             else:
-                bank = psum.tile([P, K], F32, name="dxp", tag="dxp", bufs=2)
+                bank = psum.tile([P, K], F32, name="dxp", tag="sums", bufs=2)
                 sums = [bank[:, b * P : (b + 1) * P] for b in range(K_BLOCKS)]
             for b in range(K_BLOCKS):
                 for w, (words, plane) in enumerate(((w3tw, w3ts), (w1tw, w1ts))):
@@ -213,19 +220,20 @@ def tile_moe_rec_glu_silu_kernel(
                         start=(w == 0), stop=(w == 1),
                     )
             for b in range(K_BLOCKS):
-                nc.scalar.copy(dx[b][:, j * P : (j + 1) * P], sums[b])
+                if e < E - 1:
+                    nc.scalar.copy(dx[b][:, j * P : (j + 1) * P], sums[b])
+                elif j % 2 == 1:
+                    nc.scalar.copy(dx[b][:, e * C : (e + 1) * C], last[b][:])
 
-        make_dh_sig(0)
+        make_slope(0)
         for j in range(TILES):
             make_da(j)
             if j + 1 < TILES:
-                make_dh_sig(j + 1)
+                make_slope(j + 1)
             if j > 0:
                 second_product(j - 1)
             if j + AHEAD < TILES:
                 activations(j + AHEAD)
-            if j in (1, 3):
-                gather_gradients(j // 2 + 2)
         second_product(TILES - 1)
 
         first = []

@@ -24,8 +24,7 @@ TILES = S // P
 DY_PASSES = N // 512
 K_BLOCKS = K // P
 AHEAD = 6
-HALF = S // 2
-SPARE = 192
+ON_VECTOR = 4
 
 
 def tile_moe_rec_glu_silu_kernel(
@@ -41,9 +40,9 @@ def tile_moe_rec_glu_silu_kernel(
         def held(name, cols, dtype):
             return keep.tile([P, cols], dtype, name=name, align_bytes=64)
 
-        def zeroed_plane(name, passes, engine):
+        def zeroed_plane(name, passes):
             plane = held(name, passes * 512, U8)
-            engine.memset(plane[:].bitcast(I32), 0)
+            nc.vector.memset(plane[:].bitcast(I32), 0)
             return plane
 
         def load_scales(*pairs):
@@ -66,57 +65,57 @@ def tile_moe_rec_glu_silu_kernel(
         def by_pass(packed):
             return packed.rearrange("e s a n -> (e s) a n")
 
-        xs = zeroed_plane("xs", 2, nc.vector)
-        dys = zeroed_plane("dys", 4, nc.vector)
-        w1s = zeroed_plane("w1s", E, nc.vector)
-        xw = held("xw", T + SPARE, I32)
-        nc.vector.memset(xw[:, T:], 0)
-        dyw = [held("dyw%d" % s, T + SPARE, I32) for s in range(DY_PASSES)]
-        for tile in dyw:
-            nc.vector.memset(tile[:, T:], 0)
-        w3s = zeroed_plane("w3s", E, nc.gpsimd)
+        xs = zeroed_plane("xs", 1)
+        w1s = zeroed_plane("w1s", E)
+        dys = zeroed_plane("dys", 2)
+        w3s = zeroed_plane("w3s", E)
+        w2s = zeroed_plane("w2s", E * DY_PASSES)
+        dysg1 = zeroed_plane("dysg1", 2)
+        w1ts = zeroed_plane("w1ts", E)
+        w3ts = zeroed_plane("w3ts", E)
         gate_rows = held("gate_rows", P, F32)
         nc.gpsimd.memset(gate_rows[:], 0.0)
-        w2s = zeroed_plane("w2s", E * DY_PASSES, nc.gpsimd)
         ident = held("ident", P, F32)
         make_identity(nc, ident[:])
-        dysg1 = zeroed_plane("dysg1", 2, nc.gpsimd)
-        w1ts = zeroed_plane("w1ts", E, nc.gpsimd)
-        w3ts = zeroed_plane("w3ts", E, nc.gpsimd)
+        xw = held("xw", T, I32)
+        dyw = [held("dyw%d" % s, T, I32) for s in range(DY_PASSES)]
 
         offs_sb = keep.tile([P, S // 16], U16, name="offs_sb")
         nc.sync.dma_start(offs_sb[:], offs)
-        nc.sync.dma_start(out=xw[:, 0:T], in_=x_words[0].rearrange("p t d -> p (t d)").bitcast(I32))
-        load_scales((xs[:, 0:T], x_scales))
+        nc.sync.dma_start(out=xw[:], in_=x_words[0].rearrange("p t d -> p (t d)").bitcast(I32))
+        load_scales((xs, x_scales))
+        load_scales((w1s, by_pass(w1_scales)))
         for q in range(4):
             nc.sync.dma_start(out=dys[32 * q : 32 * q + 8, 0:T].bitcast(I32),
                               in_=dy_scales[:, 4 * q : 4 * q + 4, :].bitcast(I32))
-        load_scales((w1s, by_pass(w1_scales)))
         w1w = load_words("w1w", by_pass(w1_words))
         w3w = load_words("w3w", by_pass(w3_words))
         w2w = [load_words("w2w0", by_pass(w2t_words)[0:4])]
         for s in range(DY_PASSES):
-            nc.sync.dma_start(out=dyw[s][:, 0:T], in_=dy_words[s].rearrange("p t d -> p (t d)").bitcast(I32))
+            nc.sync.dma_start(out=dyw[s][:], in_=dy_words[s].rearrange("p t d -> p (t d)").bitcast(I32))
         nc.sync.dma_start(out=gate_rows[0:TILES, :], in_=gate[0].rearrange("(j p) -> j p", p=P))
         load_scales((w3s, by_pass(w3_scales)))
         load_scales((w2s, by_pass(w2t_scales)))
 
-        def gathered(name, window, dtype, first_slot, slots):
-            tile = held(name, slots, dtype)
-            nc.vector.tensor_copy(tile[:], window.indirect(offs_sb[:, first_slot // 16 : (first_slot + slots) // 16]))
-            return tile
+        def gather(dest, window, first_slot):
+            slots = dest.shape[1]
+            nc.vector.tensor_copy(dest, window.indirect(offs_sb[:, first_slot // 16 : (first_slot + slots) // 16]))
 
-        xg, xsg, dyg = [], [], []
-        for a in range(2):
-            xg.append(gathered("xg%d" % a, xw[:].bitcast(U32), U32, a * HALF, HALF))
-            xsg.append(gathered("xsg%d" % a, xs[:], U8, a * HALF, HALF))
-        dysg0 = gathered("dysg0", dys[:], U8, 0, S)
+        xg = [held("xg%d" % e, C, U32) for e in range(E)]
+        xsg = [held("xsg%d" % e, C, U8) for e in range(E)]
+        for e in range(E):
+            gather(xg[e][:], xw[:].bitcast(U32), e * C)
+            gather(xsg[e][:], xs[:], e * C)
+        dysg0 = held("dysg0", S, U8)
+        for first_slot in range(0, S, T):
+            gather(dysg0[:, first_slot : first_slot + T], dys[:], first_slot)
         for r in range(4):
             nc.sync.dma_start(out=dysg1[r:P:32, :].bitcast(I32), in_=dysg0[4 + r : P : 32, :].bitcast(I32))
-        for a in range(2):
-            dyg.append([gathered("dyg%d_%d" % (a, s), dyw[s][:].bitcast(U32), U32, a * HALF, HALF)
-                        for s in range(DY_PASSES)])
-        dysg = [[plane[:, a * HALF : (a + 1) * HALF] for plane in (dysg0, dysg1)] for a in range(2)]
+        dyg = [[held("dyg%d_%d" % (e, s), C, U32) for s in range(DY_PASSES)] for e in range(E)]
+        for e in range(E):
+            for s in range(DY_PASSES):
+                gather(dyg[e][s][:], dyw[s][:].bitcast(U32), e * C)
+        dysg = [[plane[:, e * C : (e + 1) * C] for plane in (dysg0, dysg1)] for e in range(E)]
 
         w2w.append(load_words("w2w1", by_pass(w2t_words)[4:8]))
         load_scales((w1ts, by_pass(w1t_scales)), (w3ts, by_pass(w3t_scales)))
@@ -128,24 +127,33 @@ def tile_moe_rec_glu_silu_kernel(
         nc.sync.dma_start(pos2_sb[:], pos2)
 
         def first_product(bank, codes, scales, j, words, plane, g, start, stop):
-            cols = slice((j % 4) * P, (j % 4 + 1) * P)
+            cols = slice((j % 2) * P, (j % 2 + 1) * P)
             nc.tensor.matmul_mx(
                 out=bank[:], lhsT=codes[:, cols].bitcast(FP8X4), lhsT_scale=scales[:, cols],
                 rhs=words.bitcast(FP4X4), rhs_scale=plane[:, g * 512 : (g + 1) * 512], start=start, stop=stop,
             )
 
-        silu, sneg = {}, {}
+        def by_pair(bank):
+            return bank[:].rearrange("p (m u e) -> p u m e", u=2, e=2)
+
+        def in_pairs(tile):
+            return tile[:].rearrange("p (u m e) -> p u m e", u=2, e=2)
+
+        silu, sneg, silu_less_one = {}, {}, {}
 
         def activations(j):
             e = j // 2
             a1 = psum.tile([P, H], F32, name="a1", tag="sums", bufs=2)
-            first_product(a1, xg[j // 4], xsg[j // 4], j, w1w[:, e * 1024 : (e + 1) * 1024], w1s, e, True, True)
+            first_product(a1, xg[e], xsg[e], j, w1w[:, e * 1024 : (e + 1) * 1024], w1s, e, True, True)
             silu[j] = held("silu%d" % j, H, F32)
-            nc.scalar.activation(silu[j][:], a1[:], ACT.Silu)
+            nc.scalar.activation(in_pairs(silu[j]), by_pair(a1), ACT.Silu)
             th = ring.tile([P, H], F32, name="th")
-            nc.scalar.activation(th[:], a1[:], ACT.Tanh, scale=0.5)
+            nc.scalar.activation(in_pairs(th), by_pair(a1), ACT.Tanh, scale=0.5)
             sneg[j] = held("sneg%d" % j, H, F32)
             nc.scalar.activation(sneg[j][:], th[:], ACT.Copy, scale=-0.5, bias=0.5)
+            if j >= ON_VECTOR:
+                silu_less_one[j] = held("silu_less_one%d" % j, H, F32)
+                nc.scalar.activation(silu_less_one[j][:], silu[j][:], ACT.Copy, bias=-1.0)
 
         gate_ps = psum.tile([P, 4, P], F32, name="gate_ps", tag="turn", bufs=2)
         nc.tensor.transpose(gate_ps[:, 0, :], gate_rows[:], ident[:])
@@ -156,38 +164,47 @@ def tile_moe_rec_glu_silu_kernel(
             activations(j)
 
         dx = [held("dx%d" % b, S, F32) for b in range(K_BLOCKS)]
-        slope, grouped, last = {}, {}, []
+        slope, grouped, banks = {}, {}, {}
 
         def make_slope(j):
-            slope[j] = ring.tile([P, H], F32, name="slope")
-            nc.vector.scalar_tensor_tensor(slope[j][:], silu[j][:], -1.0, sneg[j][:], ALU.add, ALU.mult)
+            slope[j] = ring.tile([P, H], F32, name="slope", bufs=2)
+            if j >= ON_VECTOR:
+                nc.gpsimd.tensor_tensor(slope[j][:], silu_less_one[j][:], sneg[j][:], ALU.mult)
+            else:
+                nc.vector.scalar_tensor_tensor(slope[j][:], silu[j][:], -1.0, sneg[j][:], ALU.add, ALU.mult)
 
         def make_da(j):
             e = j // 2
             a3 = psum.tile([P, H], F32, name="a3", tag="a3", bufs=2)
-            first_product(a3, xg[j // 4], xsg[j // 4], j, w3w[:, e * 1024 : (e + 1) * 1024], w3s, e, True, True)
+            first_product(a3, xg[e], xsg[e], j, w3w[:, e * 1024 : (e + 1) * 1024], w3s, e, True, True)
             dh = psum.tile([P, H], F32, name="dh", tag="dh", bufs=2)
             for s in range(DY_PASSES):
                 g = e * DY_PASSES + s
-                first_product(dh, dyg[j // 4][s], dysg[j // 4][s], j, w2w[g // 4][:, (g % 4) * 1024 : (g % 4 + 1) * 1024],
+                first_product(dh, dyg[e][s], dysg[e][s], j, w2w[g // 4][:, (g % 4) * 1024 : (g % 4 + 1) * 1024],
                               w2s, g, s == 0, s == DY_PASSES - 1)
             up = ring.tile([P, H], F32, name="up")
-            nc.vector.scalar_tensor_tensor(up[:], slope[j][:], 1.0, a3[:], ALU.add, ALU.mult)
             da3 = ring.tile([P, H], BF16, name="da3")
-            nc.vector.scalar_tensor_tensor(da3[:], dh[:], gate_col[:, j : j + 1], silu[j][:], ALU.mult, ALU.mult)
             da1 = ring.tile([P, H], BF16, name="da1")
-            nc.vector.scalar_tensor_tensor(da1[:], dh[:], gate_col[:, j : j + 1], up[:], ALU.mult, ALU.mult)
-            parts = [[da3], [da1]] if j == TILES - 1 else [[da3, da1]]
-            grouped[j] = [turn_and_group(part) for part in parts]
+            for u in range(2):
+                nc.vector.scalar_tensor_tensor(in_pairs(up)[:, u], in_pairs(slope[j])[:, u], 1.0, by_pair(a3)[:, u],
+                                               ALU.add, ALU.mult)
+            for da, factor in ((da3, silu[j]), (da1, up)):
+                for u in range(2):
+                    nc.vector.scalar_tensor_tensor(in_pairs(da)[:, u], by_pair(dh)[:, u], gate_col[:, j : j + 1],
+                                                   in_pairs(factor)[:, u], ALU.mult, ALU.mult)
+            if j == TILES - 1:
+                grouped[j] = [turn_and_group([da], nc.vector.tensor_copy) for da in (da3, da1)]
+            else:
+                grouped[j] = [turn_and_group([da3, da1], nc.scalar.copy)]
 
-        def turn_and_group(part):
+        def turn_and_group(part, copy):
             n = len(part)
             turn = psum.tile([P, 2 * n, P], F32, name="turn", tag="turn", bufs=2)
             for w, da in enumerate(part):
                 for u in range(2):
-                    nc.tensor.transpose(turn[:, 2 * w + u, :], da[:].bitcast(F32)[:, u : H // 2 : 2], ident[:])
+                    nc.tensor.transpose(turn[:, 2 * w + u, :], da[:].bitcast(F32)[:, u * P : (u + 1) * P], ident[:])
             group = ring.tile([P, n * 4 * P], BF16, name="group", align_bytes=64)
-            nc.scalar.copy(
+            copy(
                 group[:].bitcast(F32).rearrange("p (w s u) -> p w s u", w=n, u=2),
                 turn[:].rearrange("p (w u) s -> p w s u", u=2),
             )
@@ -202,14 +219,13 @@ def tile_moe_rec_glu_silu_kernel(
                 scales = ring.tile([P, width], U8, name="scales", align_bytes=64)
                 nc.vector.quantize_mx(out=codes[:].bitcast(FP8X4), scales=scales[:], in_=group[:])
                 operands.extend((codes[:, c : c + P], scales[:, c : c + P]) for c in range(0, width, P))
-            if e == E - 1:
-                if j % 2 == 0:
-                    last.extend(psum.tile([P, C], F32, name="last", tag=tag, bufs=bufs)
-                                for tag, bufs in (("a3", 2), ("a3", 2), ("dh", 2), ("sums", 2)))
-                sums = [bank[:, (j % 2) * P : (j % 2 + 1) * P] for bank in last]
-            else:
-                bank = psum.tile([P, K], F32, name="dxp", tag="sums", bufs=2)
-                sums = [bank[:, b * P : (b + 1) * P] for b in range(K_BLOCKS)]
+            if j % 2 == 0:
+                if e == E - 1:
+                    banks[e] = [psum.tile([P, C], F32, name="last", tag=tag, bufs=2)[:] for tag in ("a3", "a3", "dh", "sums")]
+                else:
+                    pair = [psum.tile([P, 2 * C], F32, name="dxp", tag="sums", bufs=2) for a in range(2)]
+                    banks[e] = [pair[b // 2][:, (b % 2) * C : (b % 2 + 1) * C] for b in range(K_BLOCKS)]
+            sums = [bank[:, (j % 2) * P : (j % 2 + 1) * P] for bank in banks[e]]
             for b in range(K_BLOCKS):
                 for w, (words, plane) in enumerate(((w3tw, w3ts), (w1tw, w1ts))):
                     nc.tensor.matmul_mx(
@@ -219,21 +235,19 @@ def tile_moe_rec_glu_silu_kernel(
                         rhs=operands[w][0].bitcast(FP8X4), rhs_scale=operands[w][1],
                         start=(w == 0), stop=(w == 1),
                     )
-            for b in range(K_BLOCKS):
-                if e < E - 1:
-                    nc.scalar.copy(dx[b][:, j * P : (j + 1) * P], sums[b])
-                elif j % 2 == 1:
-                    nc.scalar.copy(dx[b][:, e * C : (e + 1) * C], last[b][:])
+            if j % 2 == 1:
+                for b in range(K_BLOCKS):
+                    nc.scalar.copy(dx[b][:, e * C : (e + 1) * C], banks[e][b])
 
         make_slope(0)
         for j in range(TILES):
             make_da(j)
             if j + 1 < TILES:
                 make_slope(j + 1)
-            if j > 0:
-                second_product(j - 1)
             if j + AHEAD < TILES:
                 activations(j + AHEAD)
+            if j > 0:
+                second_product(j - 1)
         second_product(TILES - 1)
 
         first = []

@@ -6,7 +6,7 @@ from concourse.masks import make_identity
 K, T, E, C, H, N = 512, 512, 4, 256, 512, 1024
 S = E * C
 FLOPS = 2 * S * (2 * K * H + N * H + 2 * H * K)
-BYTES = 5238784
+BYTES = (K + N) * T * 33 // 32 + E * (4 * K + N) * H * 17 // 32 + 4 * S + 256 * (S + 2 * T) // 16 + 4 * K * T
 
 F32 = mybir.dt.float32
 BF16 = mybir.dt.bfloat16
@@ -20,11 +20,15 @@ ACT = mybir.ActivationFunctionType
 ALU = mybir.AluOpType
 
 P = 128
+COLS = 512
+FP4_ROW = 2 * COLS
 TILES = S // P
+LAST = TILES - 1
 DY_PASSES = N // 512
 K_BLOCKS = K // P
 AHEAD = 6
-ON_VECTOR = 4
+SLOPE_ON_VECTOR = 3
+LAST_PIECES = (384, 128)
 
 
 def tile_moe_rec_glu_silu_kernel(
@@ -35,13 +39,13 @@ def tile_moe_rec_glu_silu_kernel(
     with ExitStack() as ctx:
         keep = ctx.enter_context(tc.tile_pool(name="keep", bufs=1))
         ring = ctx.enter_context(tc.tile_pool(name="ring", bufs=3))
-        psum = ctx.enter_context(tc.psum_pool(name="psum", bufs=1))
+        psum = ctx.enter_context(tc.psum_pool(name="psum", bufs=2))
 
         def held(name, cols, dtype):
             return keep.tile([P, cols], dtype, name=name, align_bytes=64)
 
-        def zeroed_plane(name, passes):
-            plane = held(name, passes * 512, U8)
+        def zeroed_plane(name, cols):
+            plane = held(name, cols, U8)
             nc.vector.memset(plane[:].bitcast(I32), 0)
             return plane
 
@@ -49,15 +53,14 @@ def tile_moe_rec_glu_silu_kernel(
             for r in range(4):
                 for plane, scales in pairs:
                     nc.sync.dma_start(
-                        out=plane[r:P:32, :].bitcast(I32).rearrange("q (g n) -> q g n", n=128),
+                        out=plane[r:P:32, :].bitcast(I32).rearrange("q (g n) -> q g n", n=COLS // 4),
                         in_=scales[:, r:16:4, :].bitcast(I32).rearrange("g q n -> q g n"),
                     )
 
         def load_words(name, words):
-            passes = words.shape[0]
-            tile = held(name, passes * 1024, U8)
+            tile = held(name, words.shape[0] * FP4_ROW, U8)
             nc.sync.dma_start(
-                out=tile[:].bitcast(I32).rearrange("p (g n) -> p g n", n=256),
+                out=tile[:].bitcast(I32).rearrange("p (g n) -> p g n", n=FP4_ROW // 4),
                 in_=words.bitcast(I32).rearrange("g p n -> p g n"),
             )
             return tile
@@ -65,14 +68,14 @@ def tile_moe_rec_glu_silu_kernel(
         def by_pass(packed):
             return packed.rearrange("e s a n -> (e s) a n")
 
-        xs = zeroed_plane("xs", 1)
-        w1s = zeroed_plane("w1s", E)
-        dys = zeroed_plane("dys", 2)
-        w3s = zeroed_plane("w3s", E)
-        w2s = zeroed_plane("w2s", E * DY_PASSES)
-        dysg1 = zeroed_plane("dysg1", 2)
-        w1ts = zeroed_plane("w1ts", E)
-        w3ts = zeroed_plane("w3ts", E)
+        xs = zeroed_plane("xs", COLS)
+        w1s = zeroed_plane("w1s", E * COLS)
+        dys = zeroed_plane("dys", 2 * T)
+        w3s = zeroed_plane("w3s", E * COLS)
+        w2s = zeroed_plane("w2s", E * DY_PASSES * COLS)
+        dysg1 = zeroed_plane("dysg1", S)
+        w1ts = zeroed_plane("w1ts", E * COLS)
+        w3ts = zeroed_plane("w3ts", E * COLS)
         gate_rows = held("gate_rows", P, F32)
         nc.gpsimd.memset(gate_rows[:], 0.0)
         ident = held("ident", P, F32)
@@ -90,7 +93,7 @@ def tile_moe_rec_glu_silu_kernel(
                               in_=dy_scales[:, 4 * q : 4 * q + 4, :].bitcast(I32))
         w1w = load_words("w1w", by_pass(w1_words))
         w3w = load_words("w3w", by_pass(w3_words))
-        w2w = [load_words("w2w0", by_pass(w2t_words)[0:4])]
+        w2w = [load_words("w2w0", by_pass(w2t_words)[0:E])]
         for s in range(DY_PASSES):
             nc.sync.dma_start(out=dyw[s][:], in_=dy_words[s].rearrange("p t d -> p (t d)").bitcast(I32))
         nc.sync.dma_start(out=gate_rows[0:TILES, :], in_=gate[0].rearrange("(j p) -> j p", p=P))
@@ -117,7 +120,7 @@ def tile_moe_rec_glu_silu_kernel(
                 gather(dyg[e][s][:], dyw[s][:].bitcast(U32), e * C)
         dysg = [[plane[:, e * C : (e + 1) * C] for plane in (dysg0, dysg1)] for e in range(E)]
 
-        w2w.append(load_words("w2w1", by_pass(w2t_words)[4:8]))
+        w2w.append(load_words("w2w1", by_pass(w2t_words)[E : 2 * E]))
         load_scales((w1ts, by_pass(w1t_scales)), (w3ts, by_pass(w3t_scales)))
         w1tw = load_words("w1tw", by_pass(w1t_words))
         w3tw = load_words("w3tw", by_pass(w3t_words))
@@ -126,92 +129,91 @@ def tile_moe_rec_glu_silu_kernel(
         pos2_sb = keep.tile([P, T // 16], U16, name="pos2_sb")
         nc.sync.dma_start(pos2_sb[:], pos2)
 
-        def first_product(bank, codes, scales, j, words, plane, g, start, stop):
-            cols = slice((j % 2) * P, (j % 2 + 1) * P)
+        def first_product(bank, j, codes, scales, words, words_pass, plane, plane_pass, start, stop):
+            slots = slice((j % 2) * P, (j % 2 + 1) * P)
             nc.tensor.matmul_mx(
-                out=bank[:], lhsT=codes[:, cols].bitcast(FP8X4), lhsT_scale=scales[:, cols],
-                rhs=words.bitcast(FP4X4), rhs_scale=plane[:, g * 512 : (g + 1) * 512], start=start, stop=stop,
+                out=bank[:], lhsT=codes[:, slots].bitcast(FP8X4), lhsT_scale=scales[:, slots],
+                rhs=words[:, words_pass * FP4_ROW : (words_pass + 1) * FP4_ROW].bitcast(FP4X4),
+                rhs_scale=plane[:, plane_pass * COLS : (plane_pass + 1) * COLS], start=start, stop=stop,
             )
 
         def by_pair(bank):
-            return bank[:].rearrange("p (m u e) -> p u m e", u=2, e=2)
+            return bank[:].rearrange("p (m u v) -> p u m v", u=2, v=2)
 
         def in_pairs(tile):
-            return tile[:].rearrange("p (u m e) -> p u m e", u=2, e=2)
+            return tile[:].rearrange("p (u m v) -> p u m v", u=2, v=2)
 
-        silu, sneg, silu_less_one = {}, {}, {}
+        silu, sig_neg, silu_less_one = {}, {}, {}
 
         def activations(j):
             e = j // 2
-            a1 = psum.tile([P, H], F32, name="a1", tag="sums", bufs=2)
-            first_product(a1, xg[e], xsg[e], j, w1w[:, e * 1024 : (e + 1) * 1024], w1s, e, True, True)
+            a1 = psum.tile([P, H], F32, name="a1", tag="sums")
+            first_product(a1, j, xg[e], xsg[e], w1w, e, w1s, e, True, True)
             silu[j] = held("silu%d" % j, H, F32)
             nc.scalar.activation(in_pairs(silu[j]), by_pair(a1), ACT.Silu)
-            th = ring.tile([P, H], F32, name="th")
-            nc.scalar.activation(in_pairs(th), by_pair(a1), ACT.Tanh, scale=0.5)
-            sneg[j] = held("sneg%d" % j, H, F32)
-            nc.scalar.activation(sneg[j][:], th[:], ACT.Copy, scale=-0.5, bias=0.5)
-            if j >= ON_VECTOR:
+            tanh_half = ring.tile([P, H], F32, name="tanh_half")
+            nc.scalar.activation(in_pairs(tanh_half), by_pair(a1), ACT.Tanh, scale=0.5)
+            sig_neg[j] = held("sig_neg%d" % j, H, F32)
+            nc.scalar.activation(sig_neg[j][:], tanh_half[:], ACT.Copy, scale=-0.5, bias=0.5)
+            if j >= SLOPE_ON_VECTOR:
                 silu_less_one[j] = held("silu_less_one%d" % j, H, F32)
                 nc.scalar.activation(silu_less_one[j][:], silu[j][:], ACT.Copy, bias=-1.0)
 
-        gate_ps = psum.tile([P, 4, P], F32, name="gate_ps", tag="turn", bufs=2)
-        nc.tensor.transpose(gate_ps[:, 0, :], gate_rows[:], ident[:])
+        gate_turned = psum.tile([P, P], F32, name="gate_turned", tag="turn")
+        nc.tensor.transpose(gate_turned[:], gate_rows[:], ident[:])
         gate_col = held("gate_col", TILES, F32)
-        nc.vector.tensor_copy(gate_col[:], gate_ps[:, 0, 0:TILES])
+        nc.vector.tensor_copy(gate_col[:], gate_turned[:, 0:TILES])
 
         for j in range(AHEAD):
             activations(j)
 
         dx = [held("dx%d" % b, S, F32) for b in range(K_BLOCKS)]
-        slope, grouped, banks = {}, {}, {}
+        slope, grouped, dx_banks = {}, {}, {}
 
         def make_slope(j):
             slope[j] = ring.tile([P, H], F32, name="slope", bufs=2)
-            if j >= ON_VECTOR:
-                nc.gpsimd.tensor_tensor(slope[j][:], silu_less_one[j][:], sneg[j][:], ALU.mult)
+            if j >= SLOPE_ON_VECTOR:
+                nc.gpsimd.tensor_tensor(slope[j][:], silu_less_one[j][:], sig_neg[j][:], ALU.mult)
             else:
-                nc.vector.scalar_tensor_tensor(slope[j][:], silu[j][:], -1.0, sneg[j][:], ALU.add, ALU.mult)
+                nc.vector.scalar_tensor_tensor(slope[j][:], silu[j][:], -1.0, sig_neg[j][:], ALU.add, ALU.mult)
 
         def make_da(j):
             e = j // 2
-            a3 = psum.tile([P, H], F32, name="a3", tag="a3", bufs=2)
-            first_product(a3, xg[e], xsg[e], j, w3w[:, e * 1024 : (e + 1) * 1024], w3s, e, True, True)
-            dh = psum.tile([P, H], F32, name="dh", tag="dh", bufs=2)
+            a3 = psum.tile([P, H], F32, name="a3", tag="a3")
+            first_product(a3, j, xg[e], xsg[e], w3w, e, w3s, e, True, True)
+            dh = psum.tile([P, H], F32, name="dh", tag="dh")
             for s in range(DY_PASSES):
                 g = e * DY_PASSES + s
-                first_product(dh, dyg[e][s], dysg[e][s], j, w2w[g // 4][:, (g % 4) * 1024 : (g % 4 + 1) * 1024],
-                              w2s, g, s == 0, s == DY_PASSES - 1)
-            up = ring.tile([P, H], F32, name="up")
+                first_product(dh, j, dyg[e][s], dysg[e][s], w2w[g // E], g % E, w2s, g, s == 0, s == DY_PASSES - 1)
+            a3_slope = ring.tile([P, H], F32, name="a3_slope")
             da3 = ring.tile([P, H], BF16, name="da3")
             da1 = ring.tile([P, H], BF16, name="da1")
             for u in range(2):
-                nc.vector.scalar_tensor_tensor(in_pairs(up)[:, u], in_pairs(slope[j])[:, u], 1.0, by_pair(a3)[:, u],
-                                               ALU.add, ALU.mult)
-            for da, factor in ((da3, silu[j]), (da1, up)):
+                nc.vector.scalar_tensor_tensor(in_pairs(a3_slope)[:, u], in_pairs(slope[j])[:, u], 1.0,
+                                               by_pair(a3)[:, u], ALU.add, ALU.mult)
+            for da, factor in ((da3, silu[j]), (da1, a3_slope)):
                 for u in range(2):
                     nc.vector.scalar_tensor_tensor(in_pairs(da)[:, u], by_pair(dh)[:, u], gate_col[:, j : j + 1],
                                                    in_pairs(factor)[:, u], ALU.mult, ALU.mult)
-            if j == TILES - 1:
+            if j == LAST:
                 grouped[j] = [turn_and_group([da], nc.vector.tensor_copy) for da in (da3, da1)]
             else:
                 grouped[j] = [turn_and_group([da3, da1], nc.scalar.copy)]
 
-        def turn_and_group(part, copy):
-            n = len(part)
-            turn = psum.tile([P, 2 * n, P], F32, name="turn", tag="turn", bufs=2)
-            for w, da in enumerate(part):
+        def turn_and_group(das, copy):
+            turn = psum.tile([P, 2 * len(das), P], F32, name="turn", tag="turn")
+            for w, da in enumerate(das):
                 for u in range(2):
                     nc.tensor.transpose(turn[:, 2 * w + u, :], da[:].bitcast(F32)[:, u * P : (u + 1) * P], ident[:])
-            group = ring.tile([P, n * 4 * P], BF16, name="group", align_bytes=64)
+            group = ring.tile([P, len(das) * 4 * P], BF16, name="group", align_bytes=64)
             copy(
-                group[:].bitcast(F32).rearrange("p (w s u) -> p w s u", w=n, u=2),
+                group[:].bitcast(F32).rearrange("p (w s u) -> p w s u", w=len(das), u=2),
                 turn[:].rearrange("p (w u) s -> p w s u", u=2),
             )
             return group
 
         def second_product(j):
-            e = j // 2
+            e, half = divmod(j, 2)
             operands = []
             for group in grouped[j]:
                 width = group.shape[1] // 4
@@ -219,36 +221,36 @@ def tile_moe_rec_glu_silu_kernel(
                 scales = ring.tile([P, width], U8, name="scales", align_bytes=64)
                 nc.vector.quantize_mx(out=codes[:].bitcast(FP8X4), scales=scales[:], in_=group[:])
                 operands.extend((codes[:, c : c + P], scales[:, c : c + P]) for c in range(0, width, P))
-            if j % 2 == 0:
+            if half == 0:
                 if e == E - 1:
-                    banks[e] = [psum.tile([P, C], F32, name="last", tag=tag, bufs=2)[:] for tag in ("a3", "a3", "dh", "sums")]
+                    dx_banks[e] = [psum.tile([P, C], F32, name="dx_last", tag=tag)[:] for tag in ("a3", "a3", "dh", "dh")]
                 else:
-                    pair = [psum.tile([P, 2 * C], F32, name="dxp", tag="sums", bufs=2) for a in range(2)]
-                    banks[e] = [pair[b // 2][:, (b % 2) * C : (b % 2 + 1) * C] for b in range(K_BLOCKS)]
-            sums = [bank[:, (j % 2) * P : (j % 2 + 1) * P] for bank in banks[e]]
+                    pair = [psum.tile([P, 2 * C], F32, name="dx_pair", tag="sums") for a in range(2)]
+                    dx_banks[e] = [pair[b // 2][:, (b % 2) * C : (b % 2 + 1) * C] for b in range(K_BLOCKS)]
             for b in range(K_BLOCKS):
+                first_col = e * COLS + b * P
                 for w, (words, plane) in enumerate(((w3tw, w3ts), (w1tw, w1ts))):
                     nc.tensor.matmul_mx(
-                        out=sums[b],
-                        lhsT=words[:, e * 1024 + b * 256 : e * 1024 + (b + 1) * 256].bitcast(FP4X4),
-                        lhsT_scale=plane[:, e * 512 + b * P : e * 512 + (b + 1) * P],
+                        out=dx_banks[e][b][:, half * P : (half + 1) * P],
+                        lhsT=words[:, 2 * first_col : 2 * (first_col + P)].bitcast(FP4X4),
+                        lhsT_scale=plane[:, first_col : first_col + P],
                         rhs=operands[w][0].bitcast(FP8X4), rhs_scale=operands[w][1],
                         start=(w == 0), stop=(w == 1),
                     )
-            if j % 2 == 1:
+            if half == 1:
                 for b in range(K_BLOCKS):
-                    nc.scalar.copy(dx[b][:, e * C : (e + 1) * C], banks[e][b])
+                    nc.scalar.copy(dx[b][:, e * C : (e + 1) * C], dx_banks[e][b])
 
         make_slope(0)
         for j in range(TILES):
             make_da(j)
-            if j + 1 < TILES:
+            if j < LAST:
                 make_slope(j + 1)
             if j + AHEAD < TILES:
                 activations(j + AHEAD)
             if j > 0:
                 second_product(j - 1)
-        second_product(TILES - 1)
+        second_product(LAST)
 
         first = []
 
@@ -260,10 +262,11 @@ def tile_moe_rec_glu_silu_kernel(
         for b in range(K_BLOCKS):
             if b + 1 < K_BLOCKS:
                 fetch_first(b + 1)
-            pieces = 2 if b == K_BLOCKS - 1 else 1
-            width = T // pieces
-            for c in range(0, T, width):
-                total = held("total%d_%d" % (b, c), width, F32)
-                nc.vector.tensor_tensor(total[:], dx[b][:].indirect(pos2_sb[:, c // 16 : (c + width) // 16]),
-                                        first[b][:, c : c + width], ALU.add)
-                nc.sync.dma_start(out=out[b * P : (b + 1) * P, c : c + width], in_=total[:])
+            begin = 0
+            for width in LAST_PIECES if b == K_BLOCKS - 1 else (T,):
+                end = begin + width
+                total = held("total%d_%d" % (b, begin), width, F32)
+                nc.vector.tensor_tensor(total[:], dx[b][:].indirect(pos2_sb[:, begin // 16 : end // 16]),
+                                        first[b][:, begin:end], ALU.add)
+                nc.sync.dma_start(out=out[b * P : (b + 1) * P, begin:end], in_=total[:])
+                begin = end

from contextlib import ExitStack

import concourse.mybir as mybir
from concourse.masks import make_identity

K, T, E, C, H, N = 512, 512, 4, 256, 512, 1024
S = E * C
FLOPS = 2 * S * (2 * K * H + N * H + 2 * H * K)
BYTES = (K + N) * T * 33 // 32 + E * (4 * K + N) * H * 17 // 32 + 4 * S + 256 * (S + 2 * T) // 16 + 4 * K * T

F32 = mybir.dt.float32
BF16 = mybir.dt.bfloat16
I32 = mybir.dt.int32
U32 = mybir.dt.uint32
U16 = mybir.dt.uint16
U8 = mybir.dt.uint8
FP8X4 = mybir.dt.float8_e4m3fn_x4
FP4X4 = mybir.dt.float4_e2m1fn_x4
ACT = mybir.ActivationFunctionType
ALU = mybir.AluOpType

P = 128
COLS = 512
FP4_ROW = 2 * COLS
TILES = S // P
LAST = TILES - 1
DY_PASSES = N // 512
K_BLOCKS = K // P
AHEAD = 6
SLOPE_ON_VECTOR = 3
LAST_PIECES = (384, 128)


def tile_moe_rec_glu_silu_kernel(
    tc, x_words, x_scales, dy_words, dy_scales, w1_words, w1_scales, w3_words, w3_scales,
    w2t_words, w2t_scales, w1t_words, w1t_scales, w3t_words, w3t_scales, gate, offs, pos1, pos2, out,
):
    nc = tc.nc
    with ExitStack() as ctx:
        keep = ctx.enter_context(tc.tile_pool(name="keep", bufs=1))
        ring = ctx.enter_context(tc.tile_pool(name="ring", bufs=3))
        psum = ctx.enter_context(tc.psum_pool(name="psum", bufs=2))

        def held(name, cols, dtype):
            return keep.tile([P, cols], dtype, name=name, align_bytes=64)

        def zeroed_plane(name, cols):
            plane = held(name, cols, U8)
            nc.vector.memset(plane[:].bitcast(I32), 0)
            return plane

        def load_scales(*pairs):
            for r in range(4):
                for plane, scales in pairs:
                    nc.sync.dma_start(
                        out=plane[r:P:32, :].bitcast(I32).rearrange("q (g n) -> q g n", n=COLS // 4),
                        in_=scales[:, r:16:4, :].bitcast(I32).rearrange("g q n -> q g n"),
                    )

        def load_words(name, words):
            tile = held(name, words.shape[0] * FP4_ROW, U8)
            nc.sync.dma_start(
                out=tile[:].bitcast(I32).rearrange("p (g n) -> p g n", n=FP4_ROW // 4),
                in_=words.bitcast(I32).rearrange("g p n -> p g n"),
            )
            return tile

        def by_pass(packed):
            return packed.rearrange("e s a n -> (e s) a n")

        xs = zeroed_plane("xs", COLS)
        w1s = zeroed_plane("w1s", E * COLS)
        dys = zeroed_plane("dys", 2 * T)
        w3s = zeroed_plane("w3s", E * COLS)
        w2s = zeroed_plane("w2s", E * DY_PASSES * COLS)
        dysg1 = zeroed_plane("dysg1", S)
        w1ts = zeroed_plane("w1ts", E * COLS)
        w3ts = zeroed_plane("w3ts", E * COLS)
        gate_rows = held("gate_rows", P, F32)
        nc.gpsimd.memset(gate_rows[:], 0.0)
        ident = held("ident", P, F32)
        make_identity(nc, ident[:])
        xw = held("xw", T, I32)
        dyw = [held("dyw%d" % s, T, I32) for s in range(DY_PASSES)]

        offs_sb = keep.tile([P, S // 16], U16, name="offs_sb")
        nc.sync.dma_start(offs_sb[:], offs)
        nc.sync.dma_start(out=xw[:], in_=x_words[0].rearrange("p t d -> p (t d)").bitcast(I32))
        load_scales((xs, x_scales))
        load_scales((w1s, by_pass(w1_scales)))
        for q in range(4):
            nc.sync.dma_start(out=dys[32 * q : 32 * q + 8, 0:T].bitcast(I32),
                              in_=dy_scales[:, 4 * q : 4 * q + 4, :].bitcast(I32))
        w1w = load_words("w1w", by_pass(w1_words))
        w3w = load_words("w3w", by_pass(w3_words))
        w2w = [load_words("w2w0", by_pass(w2t_words)[0:E])]
        for s in range(DY_PASSES):
            nc.sync.dma_start(out=dyw[s][:], in_=dy_words[s].rearrange("p t d -> p (t d)").bitcast(I32))
        nc.sync.dma_start(out=gate_rows[0:TILES, :], in_=gate[0].rearrange("(j p) -> j p", p=P))
        load_scales((w3s, by_pass(w3_scales)))
        load_scales((w2s, by_pass(w2t_scales)))

        def gather(dest, window, first_slot):
            slots = dest.shape[1]
            nc.vector.tensor_copy(dest, window.indirect(offs_sb[:, first_slot // 16 : (first_slot + slots) // 16]))

        xg = [held("xg%d" % e, C, U32) for e in range(E)]
        xsg = [held("xsg%d" % e, C, U8) for e in range(E)]
        for e in range(E):
            gather(xg[e][:], xw[:].bitcast(U32), e * C)
            gather(xsg[e][:], xs[:], e * C)
        dysg0 = held("dysg0", S, U8)
        for first_slot in range(0, S, T):
            gather(dysg0[:, first_slot : first_slot + T], dys[:], first_slot)
        for r in range(4):
            nc.sync.dma_start(out=dysg1[r:P:32, :].bitcast(I32), in_=dysg0[4 + r : P : 32, :].bitcast(I32))
        dyg = [[held("dyg%d_%d" % (e, s), C, U32) for s in range(DY_PASSES)] for e in range(E)]
        for e in range(E):
            for s in range(DY_PASSES):
                gather(dyg[e][s][:], dyw[s][:].bitcast(U32), e * C)
        dysg = [[plane[:, e * C : (e + 1) * C] for plane in (dysg0, dysg1)] for e in range(E)]

        w2w.append(load_words("w2w1", by_pass(w2t_words)[E : 2 * E]))
        load_scales((w1ts, by_pass(w1t_scales)), (w3ts, by_pass(w3t_scales)))
        w1tw = load_words("w1tw", by_pass(w1t_words))
        w3tw = load_words("w3tw", by_pass(w3t_words))
        pos1_sb = keep.tile([P, T // 16], U16, name="pos1_sb")
        nc.sync.dma_start(pos1_sb[:], pos1)
        pos2_sb = keep.tile([P, T // 16], U16, name="pos2_sb")
        nc.sync.dma_start(pos2_sb[:], pos2)

        def first_product(bank, j, codes, scales, words, words_pass, plane, plane_pass, start, stop):
            slots = slice((j % 2) * P, (j % 2 + 1) * P)
            nc.tensor.matmul_mx(
                out=bank[:], lhsT=codes[:, slots].bitcast(FP8X4), lhsT_scale=scales[:, slots],
                rhs=words[:, words_pass * FP4_ROW : (words_pass + 1) * FP4_ROW].bitcast(FP4X4),
                rhs_scale=plane[:, plane_pass * COLS : (plane_pass + 1) * COLS], start=start, stop=stop,
            )

        def by_pair(bank):
            return bank[:].rearrange("p (m u v) -> p u m v", u=2, v=2)

        def in_pairs(tile):
            return tile[:].rearrange("p (u m v) -> p u m v", u=2, v=2)

        silu, sig_neg, silu_less_one = {}, {}, {}

        def activations(j):
            e = j // 2
            a1 = psum.tile([P, H], F32, name="a1", tag="sums")
            first_product(a1, j, xg[e], xsg[e], w1w, e, w1s, e, True, True)
            silu[j] = held("silu%d" % j, H, F32)
            nc.scalar.activation(in_pairs(silu[j]), by_pair(a1), ACT.Silu)
            tanh_half = ring.tile([P, H], F32, name="tanh_half")
            nc.scalar.activation(in_pairs(tanh_half), by_pair(a1), ACT.Tanh, scale=0.5)
            sig_neg[j] = held("sig_neg%d" % j, H, F32)
            nc.scalar.activation(sig_neg[j][:], tanh_half[:], ACT.Copy, scale=-0.5, bias=0.5)
            if j >= SLOPE_ON_VECTOR:
                silu_less_one[j] = held("silu_less_one%d" % j, H, F32)
                nc.scalar.activation(silu_less_one[j][:], silu[j][:], ACT.Copy, bias=-1.0)

        gate_turned = psum.tile([P, P], F32, name="gate_turned", tag="turn")
        nc.tensor.transpose(gate_turned[:], gate_rows[:], ident[:])
        gate_col = held("gate_col", TILES, F32)
        nc.vector.tensor_copy(gate_col[:], gate_turned[:, 0:TILES])

        for j in range(AHEAD):
            activations(j)

        dx = [held("dx%d" % b, S, F32) for b in range(K_BLOCKS)]
        slope, grouped, dx_banks = {}, {}, {}

        def make_slope(j):
            slope[j] = ring.tile([P, H], F32, name="slope", bufs=2)
            if j >= SLOPE_ON_VECTOR:
                nc.gpsimd.tensor_tensor(slope[j][:], silu_less_one[j][:], sig_neg[j][:], ALU.mult)
            else:
                nc.vector.scalar_tensor_tensor(slope[j][:], silu[j][:], -1.0, sig_neg[j][:], ALU.add, ALU.mult)

        def make_da(j):
            e = j // 2
            a3 = psum.tile([P, H], F32, name="a3", tag="a3")
            first_product(a3, j, xg[e], xsg[e], w3w, e, w3s, e, True, True)
            dh = psum.tile([P, H], F32, name="dh", tag="dh")
            for s in range(DY_PASSES):
                g = e * DY_PASSES + s
                first_product(dh, j, dyg[e][s], dysg[e][s], w2w[g // E], g % E, w2s, g, s == 0, s == DY_PASSES - 1)
            a3_slope = ring.tile([P, H], F32, name="a3_slope")
            da3 = ring.tile([P, H], BF16, name="da3")
            da1 = ring.tile([P, H], BF16, name="da1")
            for u in range(2):
                nc.vector.scalar_tensor_tensor(in_pairs(a3_slope)[:, u], in_pairs(slope[j])[:, u], 1.0,
                                               by_pair(a3)[:, u], ALU.add, ALU.mult)
            for da, factor in ((da3, silu[j]), (da1, a3_slope)):
                for u in range(2):
                    nc.vector.scalar_tensor_tensor(in_pairs(da)[:, u], by_pair(dh)[:, u], gate_col[:, j : j + 1],
                                                   in_pairs(factor)[:, u], ALU.mult, ALU.mult)
            if j == LAST:
                grouped[j] = [turn_and_group([da], nc.vector.tensor_copy) for da in (da3, da1)]
            else:
                grouped[j] = [turn_and_group([da3, da1], nc.scalar.copy)]

        def turn_and_group(das, copy):
            turn = psum.tile([P, 2 * len(das), P], F32, name="turn", tag="turn")
            for w, da in enumerate(das):
                for u in range(2):
                    nc.tensor.transpose(turn[:, 2 * w + u, :], da[:].bitcast(F32)[:, u * P : (u + 1) * P], ident[:])
            group = ring.tile([P, len(das) * 4 * P], BF16, name="group", align_bytes=64)
            copy(
                group[:].bitcast(F32).rearrange("p (w s u) -> p w s u", w=len(das), u=2),
                turn[:].rearrange("p (w u) s -> p w s u", u=2),
            )
            return group

        def second_product(j):
            e, half = divmod(j, 2)
            operands = []
            for group in grouped[j]:
                width = group.shape[1] // 4
                codes = ring.tile([P, width], U32, name="codes", align_bytes=64)
                scales = ring.tile([P, width], U8, name="scales", align_bytes=64)
                nc.vector.quantize_mx(out=codes[:].bitcast(FP8X4), scales=scales[:], in_=group[:])
                operands.extend((codes[:, c : c + P], scales[:, c : c + P]) for c in range(0, width, P))
            if half == 0:
                if e == E - 1:
                    dx_banks[e] = [psum.tile([P, C], F32, name="dx_last", tag=tag)[:] for tag in ("a3", "a3", "dh", "dh")]
                else:
                    pair = [psum.tile([P, 2 * C], F32, name="dx_pair", tag="sums") for a in range(2)]
                    dx_banks[e] = [pair[b // 2][:, (b % 2) * C : (b % 2 + 1) * C] for b in range(K_BLOCKS)]
            for b in range(K_BLOCKS):
                first_col = e * COLS + b * P
                for w, (words, plane) in enumerate(((w3tw, w3ts), (w1tw, w1ts))):
                    nc.tensor.matmul_mx(
                        out=dx_banks[e][b][:, half * P : (half + 1) * P],
                        lhsT=words[:, 2 * first_col : 2 * (first_col + P)].bitcast(FP4X4),
                        lhsT_scale=plane[:, first_col : first_col + P],
                        rhs=operands[w][0].bitcast(FP8X4), rhs_scale=operands[w][1],
                        start=(w == 0), stop=(w == 1),
                    )
            if half == 1:
                for b in range(K_BLOCKS):
                    nc.scalar.copy(dx[b][:, e * C : (e + 1) * C], dx_banks[e][b])

        make_slope(0)
        for j in range(TILES):
            make_da(j)
            if j < LAST:
                make_slope(j + 1)
            if j + AHEAD < TILES:
                activations(j + AHEAD)
            if j > 0:
                second_product(j - 1)
        second_product(LAST)

        first = []

        def fetch_first(b):
            first.append(held("first%d" % b, T, F32))
            nc.vector.tensor_copy(first[b][:], dx[b][:].indirect(pos1_sb[:]))

        fetch_first(0)
        for b in range(K_BLOCKS):
            if b + 1 < K_BLOCKS:
                fetch_first(b + 1)
            begin = 0
            for width in LAST_PIECES if b == K_BLOCKS - 1 else (T,):
                end = begin + width
                total = held("total%d_%d" % (b, begin), width, F32)
                nc.vector.tensor_tensor(total[:], dx[b][:].indirect(pos2_sb[:, begin // 16 : end // 16]),
                                        first[b][:, begin:end], ALU.add)
                nc.sync.dma_start(out=out[b * P : (b + 1) * P, begin:end], in_=total[:])
                begin = end
